import numpy as np
import ml_dtypes


def mxq(x, axis, fmt="e4m3"):
    dtype, down = {"e4m3": (ml_dtypes.float8_e4m3fn, 7), "e5m2": (ml_dtypes.float8_e5m2, 14)}[fmt]
    v = np.moveaxis(np.asarray(x, np.float32).astype(ml_dtypes.bfloat16).astype(np.float64), axis, -1)
    blocks = v.reshape(v.shape[:-1] + (-1, 32))
    amax = np.abs(blocks).max(-1, keepdims=True)
    byte = np.maximum(np.where(amax > 0, np.frexp(amax)[1] - 1 + 127, 0) - down, 1)
    scale = np.exp2(byte - 127.0)
    codes = (blocks / scale).astype(np.float32).astype(dtype).astype(np.float64)
    return np.moveaxis((codes * scale).reshape(v.shape), -1, axis)


WIDE = False


def mx_kscale(k):
    if not WIDE:
        return np.ones(k)
    levels = np.array([10, -10, 5, -5, 0])
    if k % 512:
        return np.exp2(np.random.permutation(np.resize(levels, k // 32))).repeat(32)
    a = np.empty((k // 512, 16))
    for p in range(k // 512):
        a[p, :8] = np.random.permutation(np.resize(levels, 8))
        for g in range(8):
            far = levels[np.abs(levels - a[p, g]) >= 10]
            a[p, g + 8] = far[np.random.randint(len(far))]
    return np.exp2(a.ravel()).repeat(32)


def f64(x):
    return np.asarray(x).astype(np.float64)


def striped(idx):
    return np.tile(idx.reshape(-1, 16).T, (8, 1)).astype(np.uint16)


def unstriped(offs):
    return offs[:16].T.reshape(-1).astype(np.int64)


def striped8(idx):
    return np.concatenate([x.reshape(-1, 16).T for x in idx]).astype(np.uint16)


def runs(offs, k):
    lists = np.stack([offs[16 * r : 16 * r + 16].T.reshape(-1) for r in range(8)]).astype(np.int64)
    return lists[np.arange(k) % 512 // 64]


def pack_weight(w):
    k, n = w.shape
    w = f64(np.asarray(w, np.float32).astype(ml_dtypes.bfloat16)).reshape(k // 32, 32, n)
    amax = np.abs(w).max(1)
    byte = np.clip(np.where(amax > 0, np.frexp(amax)[1] - 1 + 127 - 7, 1), 1, 254)
    scaled = (w * np.exp2(127.0 - byte)[:, None, :]).reshape(k, n).astype(np.float32)
    words = np.ascontiguousarray(scaled.reshape(k // 512, 128, 4, n).transpose(0, 1, 3, 2)).astype(ml_dtypes.float8_e4m3fn).view(np.uint8)
    return words, np.ascontiguousarray(byte.astype(np.uint8).reshape(k // 512, 16, n))


def unpack_weight(words, scales):
    g, p, n, _ = words.shape
    vals = np.ascontiguousarray(words).view(ml_dtypes.float8_e4m3fn).astype(np.float64) * np.repeat(np.exp2(scales.astype(np.float64) - 127.0), 8, axis=1)[..., None]
    return vals.transpose(0, 1, 3, 2).reshape(g * 512, n)


E2M1 = np.array([0.0, 0.5, 1.0, 1.5, 2.0, 3.0, 4.0, 6.0, -0.0, -0.5, -1.0, -1.5, -2.0, -3.0, -4.0, -6.0])


def pack_fp4(w):
    k, n = w.shape
    w = f64(np.asarray(w, np.float32).astype(ml_dtypes.bfloat16)).reshape(k // 32, 32, n)
    amax = np.abs(w).max(1)
    mant, ex = np.frexp(amax / 6.0)
    byte = np.clip(np.where(amax > 0, np.where(mant > 0.5, ex, ex - 1) + 127, 1), 1, 254)
    scaled = (w * np.exp2(127.0 - byte)[:, None, :]).reshape(k, n).astype(np.float32)
    c = np.ascontiguousarray(scaled.reshape(k // 512, 128, 4, n).transpose(0, 1, 3, 2)).astype(ml_dtypes.float4_e2m1fn).view(np.uint8) & 0xF
    words = (c[..., 0::2] | (c[..., 1::2] << 4)).reshape(k // 512, 128, 2 * n)
    return np.ascontiguousarray(words), np.ascontiguousarray(byte.astype(np.uint8).reshape(k // 512, 16, n))


def unpack_fp4(words, scales):
    g, _, n = scales.shape
    words = np.ascontiguousarray(words).reshape(g, 128, n, 2)
    nib = np.empty((g, 128, n, 4), np.uint8)
    nib[..., 0::2] = words & 0xF
    nib[..., 1::2] = words >> 4
    vals = E2M1[nib] * np.repeat(np.exp2(scales.astype(np.float64) - 127.0), 8, axis=1)[..., None]
    return vals.transpose(0, 1, 3, 2).reshape(g * 512, n)


def planes(y):
    n, m = y.shape
    v = y.astype(np.float32).astype(ml_dtypes.bfloat16).astype(np.float64).reshape(n // 32, 32, m)
    top = np.abs(v).max(1)
    byte = np.clip(np.where(top > 0, np.frexp(top)[1] - 1 + 127 - 7, 1), 1, 254)
    codes = (v * np.exp2(127.0 - byte)[:, None, :]).reshape(n, m).astype(np.float32).astype(ml_dtypes.float8_e4m3fn).view(np.uint8)
    words = codes.reshape(n // 512, 128, 4, m).transpose(0, 1, 3, 2)
    return np.ascontiguousarray(words), np.ascontiguousarray(byte.astype(np.uint8).reshape(n // 512, 16, m))


K, T, S, N, H, W = 512, 2048, 512, 512, 512, 256


def setup_inputs():
    n = np.random.standard_normal
    s = mx_kscale(K)[:, None]
    u = mx_kscale(H)
    packed_xT = pack_weight(n((K, T)) * s)
    packed_w1 = pack_fp4(n((K, H)) / np.sqrt(K) / s)
    packed_w2 = pack_fp4(n((K, H)) / np.sqrt(K) / s)
    packed_w3 = pack_fp4(n((H, N)) / np.sqrt(H) / u[:, None])
    perm = np.random.permutation(S)
    return {
        "x_words": packed_xT[0],
        "x_scales": packed_xT[1],
        "w1_words": packed_w1[0],
        "w1_scales": packed_w1[1],
        "w2_words": packed_w2[0],
        "w2_scales": packed_w2[1],
        "gn": (np.random.uniform(0.5, 1.5, (H, 1)) * u[:, None]).astype(np.float32),
        "w3_words": packed_w3[0],
        "w3_scales": packed_w3[1],
        "offs": striped(np.random.permutation(T)[:S]),
        "hz": striped8(np.random.randint(0, T, (8, S))),
        "n1": striped8(np.stack([np.random.permutation(S) for _ in range(8)])),
        "n2": striped8(np.stack([np.random.permutation(S) for _ in range(8)])),
        "n3": striped8(np.stack([np.random.permutation(S) for _ in range(8)])),
        "n4": striped8(np.stack([np.random.permutation(S) for _ in range(8)])),
        "n5": striped(perm[:W]),
        "n6": striped(perm[W:]),
    }


def reference(x_words, x_scales, w1_words, w1_scales, w2_words, w2_scales, gn, w3_words, w3_scales, offs, hz, n1, n2, n3, n4, n5, n6):
    xq = unpack_weight(x_words, x_scales)[:, unstriped(offs)]
    y = unpack_fp4(w1_words, w1_scales).T @ xq
    x_hz = unpack_weight(x_words, x_scales)[np.arange(K)[:, None], runs(hz, K)]
    d = unpack_fp4(w2_words, w2_scales).T @ x_hz
    z = f64(gn) * (np.maximum(y[np.arange(H)[:, None], runs(n1, H)] + d[np.arange(H)[:, None], runs(n3, H)], y[np.arange(H)[:, None], runs(n2, H)] + d[np.arange(H)[:, None], runs(n4, H)]))
    h = unpack_fp4(w3_words, w3_scales).T @ mxq(z, 0, "e4m3")
    pb = h[:, unstriped(n6)]
    pa = h[:, unstriped(n5)]
    rb = pb - (0.5 * pa)
    ra = np.sqrt((pa) ** 2 + (pb) ** 2 + 0.25)
    ds = np.zeros((N, S))
    ds[:, unstriped(n5)] = ra
    out = ds.copy()
    out[:, unstriped(n6)] = rb
    return (out,) + planes(out)

@@ -1,0 +1,266 @@
+from contextlib import ExitStack
+
+import concourse.mybir as mybir
+
+K, T, S, H, N, W = 512, 2048, 512, 512, 512, 256
+FLOPS = 3 * 2 * 512 * 512 * 512
+
+F32 = mybir.dt.float32
+BF16 = mybir.dt.bfloat16
+I32 = mybir.dt.int32
+U32 = mybir.dt.uint32
+U16 = mybir.dt.uint16
+U8 = mybir.dt.uint8
+FP8X4 = mybir.dt.float8_e4m3fn_x4
+FP4X4 = mybir.dt.float4_e2m1fn_x4
+ALU = mybir.AluOpType
+ACT = mybir.ActivationFunctionType
+
+P = 128
+PACK = 4
+HALF = S // 2
+LIST_COLS = HALF // 16
+
+
+def tile_picked_twhpathbpolar_none_po_kernel(
+    tc, x_words, x_scales, w1_words, w1_scales, w2_words, w2_scales, gn, w3_words, w3_scales,
+    offs, hz, n1, n2, n3, n4, n5, n6, out_0, out_1, out_2,
+):
+    nc = tc.nc
+    with ExitStack() as ctx:
+        lists = ctx.enter_context(tc.tile_pool(name="lists", bufs=1))
+        sb = ctx.enter_context(tc.tile_pool(name="sb", bufs=1))
+        psum = ctx.enter_context(tc.psum_pool(name="psum", bufs=1))
+
+        def load_list(src, name):
+            tile = lists.tile(list(src.shape), U16, name=name)
+            nc.sync.dma_start(tile[:], src)
+            return tile
+
+        def load_scale_rows(queue, src, dst):
+            rows = src[0].bitcast(I32)
+            queue.dma_start(dst.bitcast(I32), rows.unsqueeze(1).to_broadcast([16, 8, rows.shape[1]]))
+
+        def place_scale_rows(queue, plane, spread):
+            for r in range(1, 4):
+                queue.dma_start(plane[r:P:32, :].bitcast(I32), spread[8 * r : P : 32, :].bitcast(I32))
+
+        def load_words(queue, src, name, tag):
+            tile = sb.tile([P, 2 * H], U8, name=name, tag=tag, align_bytes=64)
+            queue.dma_start(tile[:].bitcast(I32), src[0].bitcast(I32))
+            return tile
+
+        def deal_scales(queue, scales, count, name):
+            dealt = sb.tile([P, count * H], U8, name=name, align_bytes=64)
+            nc.vector.tensor_copy(
+                dealt[:].rearrange("p (w t m) -> p w t m", w=count, t=PACK),
+                scales[:].rearrange("p (w m t) -> p w t m", w=count, t=PACK),
+            )
+            place_scale_rows(queue, dealt, dealt)
+            return dealt
+
+        def deal_words(words, name):
+            dealt = sb.tile([P, 2 * H], U8, name=name, align_bytes=64)
+            nc.vector.tensor_copy(
+                dealt[:].rearrange("p (t m b) -> p t m b", t=PACK, b=2),
+                words[:].rearrange("p (m t b) -> p t m b", t=PACK, b=2),
+            )
+            return dealt
+
+        def gather_plane(queue, offsets, name):
+            picked = sb.tile([P, S], U8, name=name + "_bytes", align_bytes=64)
+            nc.vector.tensor_copy(picked[:], xs[:].indirect(offsets[:]))
+            plane = sb.tile([P, S], U8, name=name + "_plane", align_bytes=64)
+            nc.vector.tensor_copy(plane[:].bitcast(I32), picked[:].bitcast(I32))
+            place_scale_rows(queue, plane, picked)
+            return plane
+
+        def product(out, weights, t, codes, scales):
+            words, planes = weights
+            nc.tensor.matmul_mx(
+                out=out,
+                lhsT=words[:, 2 * P * t : 2 * P * (t + 1)].bitcast(FP4X4),
+                lhsT_scale=planes[:, P * t : P * (t + 1)],
+                rhs=codes.bitcast(FP8X4),
+                rhs_scale=scales,
+                start=True,
+                stop=True,
+            )
+
+        w12s = sb.tile([P, 2 * H], U8, name="w12s", tag="raw_scales", align_bytes=64)
+        load_scale_rows(nc.scalar, w1_scales, w12s[:, 0:H])
+        load_scale_rows(nc.scalar, w2_scales, w12s[:, H : 2 * H])
+        xs = sb.tile([P, T], U8, name="xs", align_bytes=64)
+        load_scale_rows(nc.sync, x_scales, xs[:])
+        offs_t = load_list(offs, "offs_t")
+        hz_t = load_list(hz, "hz_t")
+        w1w = load_words(nc.scalar, w1_words, "w1w", "raw_words")
+        w2w = load_words(nc.scalar, w2_words, "w2w", "w2w")
+        xw = sb.tile([P, T], I32, name="xw", align_bytes=64)
+        nc.sync.dma_start(xw[:], x_words[0].rearrange("p c r -> p (c r)").bitcast(I32))
+        gain = sb.tile([P, PACK], F32, name="gain")
+        nc.gpsimd.dma_start(gain[:], gn.rearrange("(p t) o -> p (t o)", t=PACK))
+        n1_t = load_list(n1, "n1_t")
+        n2_t = load_list(n2, "n2_t")
+        n3_t = load_list(n3, "n3_t")
+        n4_t = load_list(n4, "n4_t")
+        n5_t = load_list(n5, "n5_t")
+        n6_t = load_list(n6, "n6_t")
+
+        sign = sb.tile([P, PACK], F32, name="sign")
+        step = sb.tile([P, PACK], F32, name="step")
+        size = sb.tile([P, PACK], F32, name="size")
+        nc.gpsimd.tensor_scalar(step[:], gain[:], 0.0, 2.0, ALU.is_ge, ALU.mult)
+        nc.gpsimd.tensor_scalar(sign[:], step[:], 1.0, -1.0, ALU.mult, ALU.add)
+        nc.gpsimd.tensor_tensor(size[:], gain[:], sign[:], ALU.mult)
+        quarter = sb.tile([P, 1], F32, name="quarter")
+        nc.gpsimd.memset(quarter[:], 0.25)
+
+        w12_planes = deal_scales(nc.scalar, w12s, 2, "w12_planes")
+        offs_plane = gather_plane(nc.scalar, offs_t, "offs")
+        w1 = (deal_words(w1w, "w1_dealt"), w12_planes[:, 0:H])
+        offs_codes = sb.tile([P, S], U32, name="offs_codes", align_bytes=64)
+        nc.vector.tensor_copy(offs_codes[:], xw[:].bitcast(U32).indirect(offs_t[:]))
+        y_ps = [psum.tile([P, S], F32, name=f"y_ps{t}", tag=f"bank{t}") for t in range(PACK)]
+        for t in range(PACK):
+            product(y_ps[t][:], w1, t, offs_codes[:], offs_plane[:])
+        w3s = sb.tile([P, H], U8, name="w3s", tag="raw_scales", align_bytes=64)
+        load_scale_rows(nc.sync, w3_scales, w3s[:])
+        w3w = load_words(nc.sync, w3_words, "w3w", "raw_words")
+        hz_plane = gather_plane(nc.sync, hz_t, "hz")
+        w2 = (deal_words(w2w, "w2_dealt"), w12_planes[:, H : 2 * H])
+        hz_codes = sb.tile([P, S], U32, name="hz_codes", align_bytes=64)
+        nc.vector.tensor_copy(hz_codes[:], xw[:].bitcast(U32).indirect(hz_t[:]))
+        d_ps = [psum.tile([P, S], F32, name=f"d_ps{t}", tag=f"bank{PACK + t}") for t in range(PACK)]
+        for t in range(PACK):
+            product(d_ps[t][:], w2, t, hz_codes[:], hz_plane[:])
+
+        y = [sb.tile([P, S], F32, name=f"y{t}") for t in range(PACK)]
+        d = [sb.tile([P, S], F32, name=f"d{t}") for t in range(PACK)]
+        h = [sb.tile([P, S], F32, name=f"h{t}") for t in range(PACK)]
+        h_ps = [psum.tile([P, S], F32, name=f"h_ps{t}", tag=f"bank{t}") for t in range(PACK)]
+        larger = [sb.tile([P, PACK, HALF], BF16, name=f"larger{half}") for half in range(2)]
+        signed = [sb.tile([P, PACK, HALF], BF16, name=f"signed{half}") for half in range(2)]
+        sums = {}
+        w3 = []
+
+        def fetch_y(half, t):
+            cols = slice(half * LIST_COLS, (half + 1) * LIST_COLS)
+            if half == 0:
+                nc.scalar.activation(y[t][:], y_ps[t][:], ACT.Copy, scale=size[:, t : t + 1])
+            ya = sb.tile([P, HALF], F32, name=f"ya{half}{t}")
+            yb = sb.tile([P, HALF], F32, name=f"yb{half}{t}")
+            nc.scalar.activation(ya[:], y[t][:].indirect(n1_t[:, cols]), ACT.Copy)
+            nc.scalar.activation(yb[:], y[t][:].indirect(n2_t[:, cols]), ACT.Copy)
+            if half == 0:
+                if t < 1:
+                    nc.vector.tensor_scalar(d[t][:], d_ps[t][:], size[:, t : t + 1], None, ALU.mult)
+                else:
+                    nc.scalar.activation(d[t][:], d_ps[t][:], ACT.Copy, scale=size[:, t : t + 1])
+            return ya, yb
+
+        def add_d(half, t, which, looked_up, offsets, on_scalar):
+            cols = slice(half * LIST_COLS, (half + 1) * LIST_COLS)
+            total = sb.tile([P, HALF], F32, name=f"sum{which}{half}{t}")
+            if on_scalar:
+                fetched = sb.tile([P, HALF], F32, name=f"d{which}{half}{t}")
+                nc.scalar.activation(fetched[:], d[t][:].indirect(offsets[:, cols]), ACT.Copy)
+                nc.vector.tensor_tensor(total[:], fetched[:], looked_up[:], ALU.add)
+            else:
+                nc.vector.tensor_tensor(total[:], d[t][:].indirect(offsets[:, cols]), looked_up[:], ALU.add)
+            sums[(half, t, which)] = total
+
+        def take_larger(half, t):
+            nc.vector.tensor_tensor(larger[half][:, t, :], sums[(half, t, "a")][:], sums[(half, t, "b")][:], ALU.max)
+
+        def apply_sign(half, t):
+            nc.vector.tensor_scalar(signed[half][:, t, :], larger[half][:, t, :], sign[:, t : t + 1], None, ALU.mult)
+
+        woven = [sb.tile([P, HALF, PACK], BF16, name=f"woven{half}", align_bytes=64) for half in range(2)]
+
+        def weave(half):
+            nc.vector.tensor_copy(
+                woven[half][:].rearrange("p (c i) t -> p c t i", i=4),
+                signed[half][:].rearrange("p t (c i) -> p c t i", i=4),
+            )
+
+        def third_product(half):
+            z_codes = sb.tile([P, HALF], U32, name=f"z_codes{half}", align_bytes=64)
+            z_plane = sb.tile([P, HALF], U8, name=f"z_plane{half}", align_bytes=64)
+            nc.vector.quantize_mx(
+                out=z_codes[:].bitcast(FP8X4), scales=z_plane[:], in_=woven[half][:].rearrange("p c t -> p (c t)")
+            )
+            for t in range(PACK):
+                product(h_ps[t][:, half * HALF : (half + 1) * HALF], w3, t, z_codes[:], z_plane[:])
+
+        units = [(half, t) for half in range(2) for t in range(PACK)]
+        for u, (half, t) in enumerate(units):
+            ya, yb = fetch_y(half, t)
+            add_d(half, t, "a", ya, n3_t, False)
+            if u > 0:
+                take_larger(*units[u - 1])
+            if u == PACK + 1:
+                third_product(0)
+            add_d(half, t, "b", yb, n4_t, t % 2 == 1)
+            if u > 0:
+                apply_sign(*units[u - 1])
+            if u == 1:
+                w3.append(deal_words(w3w, "w3_dealt"))
+            if u == 2:
+                w3.append(deal_scales(nc.sync, w3s, 1, "w3_plane")[:])
+            if u == PACK:
+                weave(0)
+            if u >= PACK + 2:
+                for tt in (2 * (u - PACK - 2), 2 * (u - PACK - 2) + 1):
+                    nc.scalar.copy(h[tt][:, 0:HALF], h_ps[tt][:, 0:HALF])
+        take_larger(*units[-1])
+        apply_sign(*units[-1])
+        weave(1)
+        third_product(1)
+
+        out_rows = out_0.rearrange("(p t) c -> p t c", t=PACK)
+        rounded = sb.tile([P, S, PACK], BF16, name="rounded", align_bytes=64)
+        pair = [sb.tile([P, 2, W], F32, name=f"pair{t}") for t in range(PACK)]
+        squares = [sb.tile([P, 2, W], F32, name=f"squares{t}") for t in range(PACK)]
+        total = [sb.tile([P, W], F32, name=f"total{t}") for t in range(PACK)]
+        root = [sb.tile([P, W], F32, name=f"root{t}") for t in range(PACK)]
+        result = [sb.tile([P, S], F32, name=f"result{t}") for t in range(PACK)]
+
+        def fetch_pair(t):
+            if t < 2:
+                nc.vector.tensor_copy(h[t][:, HALF:S], h_ps[t][:, HALF:S])
+            else:
+                nc.scalar.copy(h[t][:, HALF:S], h_ps[t][:, HALF:S])
+            nc.scalar.activation(pair[t][:, 0, :], h[t][:].indirect(n5_t[:]), ACT.Copy, scale=-0.5)
+            if t < 2:
+                nc.vector.tensor_copy(pair[t][:, 1, :], h[t][:].indirect(n6_t[:]))
+            else:
+                nc.scalar.activation(pair[t][:, 1, :], h[t][:].indirect(n6_t[:]), ACT.Copy)
+
+        def round_out(t):
+            nc.vector.tensor_copy(rounded[:, :, t], result[t][:])
+
+        fetch_pair(0)
+        for t in range(PACK):
+            if t + 1 < PACK:
+                fetch_pair(t + 1)
+            nc.vector.tensor_tensor(squares[t][:], pair[t][:], pair[t][:], ALU.mult)
+            if t > 1:
+                round_out(t - 2)
+            nc.vector.scalar_tensor_tensor(total[t][:], squares[t][:, 0, :], 4.0, squares[t][:, 1, :], ALU.mult, ALU.add)
+            nc.vector.tensor_tensor(result[t][:].indirect(n6_t[:]), pair[t][:, 1, :], pair[t][:, 0, :], ALU.add)
+            nc.scalar.activation(root[t][:], total[t][:], ACT.Sqrt, bias=quarter[:])
+            nc.scalar.activation(result[t][:].indirect(n5_t[:]), root[t][:], ACT.Copy)
+            nc.sync.dma_start(out_rows[:, t, :], result[t][:])
+        round_out(PACK - 2)
+        round_out(PACK - 1)
+
+        out_codes = sb.tile([P, S], I32, name="out_codes", align_bytes=64)
+        out_plane = sb.tile([P, S], U8, name="out_plane", align_bytes=64)
+        nc.vector.quantize_mx(
+            out=out_codes[:].bitcast(FP8X4), scales=out_plane[:], in_=rounded[:].rearrange("p c t -> p (c t)")
+        )
+        nc.sync.dma_start(out_1[0].rearrange("p c r -> p (c r)").bitcast(I32), out_codes[:])
+        for q in range(4):
+            queue = nc.scalar if q % 2 == 0 else nc.sync
+            queue.dma_start(out_2[0, 4 * q : 4 * q + 4, :].bitcast(I32), out_plane[32 * q : 32 * q + 4, :].bitcast(I32))

@@ -19,7 +19,6 @@ ACT = mybir.ActivationFunctionType
 P = 128
 PACK = 4
 HALF = S // 2
-LIST_COLS = HALF // 16
 
 
 def tile_picked_twhpathbpolar_none_po_kernel(
@@ -67,40 +66,38 @@ def tile_picked_twhpathbpolar_none_po_kernel(
             )
             return dealt
 
-        def gather_plane(queue, offsets, name):
+        def gather_plane(offsets, name):
             picked = sb.tile([P, S], U8, name=name + "_bytes", align_bytes=64)
             nc.vector.tensor_copy(picked[:], xs[:].indirect(offsets[:]))
             plane = sb.tile([P, S], U8, name=name + "_plane", align_bytes=64)
             nc.vector.tensor_copy(plane[:].bitcast(I32), picked[:].bitcast(I32))
-            place_scale_rows(queue, plane, picked)
+            place_scale_rows(nc.sync, plane, picked)
             return plane
 
-        def product(out, weights, t, codes, scales):
-            words, planes = weights
+        def product(out, words, plane, t, codes, scales):
             nc.tensor.matmul_mx(
                 out=out,
                 lhsT=words[:, 2 * P * t : 2 * P * (t + 1)].bitcast(FP4X4),
-                lhsT_scale=planes[:, P * t : P * (t + 1)],
+                lhsT_scale=plane[:, P * t : P * (t + 1)],
                 rhs=codes.bitcast(FP8X4),
                 rhs_scale=scales,
                 start=True,
                 stop=True,
             )
 
-        w12s = sb.tile([P, 2 * H], U8, name="w12s", tag="raw_scales", align_bytes=64)
-        load_scale_rows(nc.scalar, w1_scales, w12s[:, 0:H])
-        load_scale_rows(nc.scalar, w2_scales, w12s[:, H : 2 * H])
         xs = sb.tile([P, T], U8, name="xs", align_bytes=64)
         load_scale_rows(nc.sync, x_scales, xs[:])
+        w12s = sb.tile([P, 2 * H], U8, name="w12s", tag="raw_scales", align_bytes=64)
+        load_scale_rows(nc.scalar, w1_scales, w12s[:, 0:H])
         offs_t = load_list(offs, "offs_t")
+        load_scale_rows(nc.scalar, w2_scales, w12s[:, H : 2 * H])
         hz_t = load_list(hz, "hz_t")
         w1w = load_words(nc.scalar, w1_words, "w1w", "raw_words")
-        w2w = load_words(nc.scalar, w2_words, "w2w", "w2w")
+        n1_t = load_list(n1, "n1_t")
         xw = sb.tile([P, T], I32, name="xw", align_bytes=64)
         nc.sync.dma_start(xw[:], x_words[0].rearrange("p c r -> p (c r)").bitcast(I32))
         gain = sb.tile([P, PACK], F32, name="gain")
         nc.gpsimd.dma_start(gain[:], gn.rearrange("(p t) o -> p (t o)", t=PACK))
-        n1_t = load_list(n1, "n1_t")
         n2_t = load_list(n2, "n2_t")
         n3_t = load_list(n3, "n3_t")
         n4_t = load_list(n4, "n4_t")
@@ -116,105 +113,106 @@ def tile_picked_twhpathbpolar_none_po_kernel(
         quarter = sb.tile([P, 1], F32, name="quarter")
         nc.gpsimd.memset(quarter[:], 0.25)
 
+        y = [sb.tile([P, 2 * S], F32, name=f"y{t}") for t in range(PACK)]
+        d = [sb.tile([P, 2 * S], F32, name=f"d{t}") for t in range(PACK)]
+
         w12_planes = deal_scales(nc.scalar, w12s, 2, "w12_planes")
-        offs_plane = gather_plane(nc.scalar, offs_t, "offs")
-        w1 = (deal_words(w1w, "w1_dealt"), w12_planes[:, 0:H])
+        offs_plane = gather_plane(offs_t, "offs")
+        hz_plane = gather_plane(hz_t, "hz")
+        w1_dealt = deal_words(w1w, "w1_dealt")
+        w2w = load_words(nc.sync, w2_words, "w2w", "raw_words")
         offs_codes = sb.tile([P, S], U32, name="offs_codes", align_bytes=64)
         nc.vector.tensor_copy(offs_codes[:], xw[:].bitcast(U32).indirect(offs_t[:]))
         y_ps = [psum.tile([P, S], F32, name=f"y_ps{t}", tag=f"bank{t}") for t in range(PACK)]
         for t in range(PACK):
-            product(y_ps[t][:], w1, t, offs_codes[:], offs_plane[:])
-        w3s = sb.tile([P, H], U8, name="w3s", tag="raw_scales", align_bytes=64)
-        load_scale_rows(nc.sync, w3_scales, w3s[:])
-        w3w = load_words(nc.sync, w3_words, "w3w", "raw_words")
-        hz_plane = gather_plane(nc.sync, hz_t, "hz")
-        w2 = (deal_words(w2w, "w2_dealt"), w12_planes[:, H : 2 * H])
+            product(y_ps[t][:], w1_dealt, w12_planes[:, 0:H], t, offs_codes[:], offs_plane[:])
+        w2_dealt = deal_words(w2w, "w2_dealt")
         hz_codes = sb.tile([P, S], U32, name="hz_codes", align_bytes=64)
         nc.vector.tensor_copy(hz_codes[:], xw[:].bitcast(U32).indirect(hz_t[:]))
         d_ps = [psum.tile([P, S], F32, name=f"d_ps{t}", tag=f"bank{PACK + t}") for t in range(PACK)]
         for t in range(PACK):
-            product(d_ps[t][:], w2, t, hz_codes[:], hz_plane[:])
+            product(d_ps[t][:], w2_dealt, w12_planes[:, H : 2 * H], t, hz_codes[:], hz_plane[:])
+        w3s = sb.tile([P, H], U8, name="w3s", tag="raw_scales", align_bytes=64)
+        load_scale_rows(nc.sync, w3_scales, w3s[:])
+        w3w = load_words(nc.sync, w3_words, "w3w", "raw_words")
+        w3_plane = deal_scales(nc.sync, w3s, 1, "w3_plane")
+        w3_dealt = deal_words(w3w, "w3_dealt")
 
-        y = [sb.tile([P, S], F32, name=f"y{t}") for t in range(PACK)]
-        d = [sb.tile([P, S], F32, name=f"d{t}") for t in range(PACK)]
         h = [sb.tile([P, S], F32, name=f"h{t}") for t in range(PACK)]
         h_ps = [psum.tile([P, S], F32, name=f"h_ps{t}", tag=f"bank{t}") for t in range(PACK)]
-        larger = [sb.tile([P, PACK, HALF], BF16, name=f"larger{half}") for half in range(2)]
-        signed = [sb.tile([P, PACK, HALF], BF16, name=f"signed{half}") for half in range(2)]
+        larger = sb.tile([P, PACK, S], BF16, name="larger")
+        signed = sb.tile([P, PACK, S], BF16, name="signed")
+        woven = sb.tile([P, S, PACK], BF16, name="woven", align_bytes=64)
+        z_codes = sb.tile([P, S], U32, name="z_codes", align_bytes=64)
+        z_planes = [sb.tile([P, HALF], U8, name=f"z_plane{half}", align_bytes=64) for half in range(2)]
         sums = {}
-        w3 = []
 
-        def fetch_y(half, t):
-            cols = slice(half * LIST_COLS, (half + 1) * LIST_COLS)
-            if half == 0:
-                nc.scalar.activation(y[t][:], y_ps[t][:], ACT.Copy, scale=size[:, t : t + 1])
-            ya = sb.tile([P, HALF], F32, name=f"ya{half}{t}")
-            yb = sb.tile([P, HALF], F32, name=f"yb{half}{t}")
-            nc.scalar.activation(ya[:], y[t][:].indirect(n1_t[:, cols]), ACT.Copy)
-            nc.scalar.activation(yb[:], y[t][:].indirect(n2_t[:, cols]), ACT.Copy)
-            if half == 0:
-                if t < 1:
-                    nc.vector.tensor_scalar(d[t][:], d_ps[t][:], size[:, t : t + 1], None, ALU.mult)
-                else:
-                    nc.scalar.activation(d[t][:], d_ps[t][:], ACT.Copy, scale=size[:, t : t + 1])
-            return ya, yb
+        def entries(offsets, lo, hi):
+            return offsets[:, lo // 16 : hi // 16]
 
-        def add_d(half, t, which, looked_up, offsets, on_scalar):
-            cols = slice(half * LIST_COLS, (half + 1) * LIST_COLS)
-            total = sb.tile([P, HALF], F32, name=f"sum{which}{half}{t}")
+        def leave_psum(dst, src, t, on_vector):
+            if on_vector:
+                nc.vector.tensor_scalar(dst[:, 0:S], src[:], size[:, t : t + 1], None, ALU.mult)
+            else:
+                nc.scalar.activation(dst[:, 0:S], src[:], ACT.Copy, scale=size[:, t : t + 1])
+
+        def fetch(window, offsets, lo, hi, name):
+            fetched = sb.tile([P, hi - lo], F32, name=name)
+            nc.scalar.activation(fetched[:], window[:].indirect(entries(offsets, lo, hi)), ACT.Copy)
+            return fetched
+
+        def add_d(t, lo, hi, which, looked_up, offsets, on_scalar):
+            total = sb.tile([P, hi - lo], F32, name=f"sum{which}{t}_{lo}")
             if on_scalar:
-                fetched = sb.tile([P, HALF], F32, name=f"d{which}{half}{t}")
-                nc.scalar.activation(fetched[:], d[t][:].indirect(offsets[:, cols]), ACT.Copy)
+                fetched = fetch(d[t], offsets, lo, hi, f"d{which}{t}_{lo}")
                 nc.vector.tensor_tensor(total[:], fetched[:], looked_up[:], ALU.add)
             else:
-                nc.vector.tensor_tensor(total[:], d[t][:].indirect(offsets[:, cols]), looked_up[:], ALU.add)
-            sums[(half, t, which)] = total
+                nc.vector.tensor_tensor(total[:], d[t][:].indirect(entries(offsets, lo, hi)), looked_up[:], ALU.add)
+            sums[(t, lo, which)] = total
 
-        def take_larger(half, t):
-            nc.vector.tensor_tensor(larger[half][:, t, :], sums[(half, t, "a")][:], sums[(half, t, "b")][:], ALU.max)
+        def take_larger(t, lo, hi):
+            nc.vector.tensor_tensor(larger[:, t, lo:hi], sums[(t, lo, "a")][:], sums[(t, lo, "b")][:], ALU.max)
 
-        def apply_sign(half, t):
-            nc.vector.tensor_scalar(signed[half][:, t, :], larger[half][:, t, :], sign[:, t : t + 1], None, ALU.mult)
-
-        woven = [sb.tile([P, HALF, PACK], BF16, name=f"woven{half}", align_bytes=64) for half in range(2)]
+        def apply_sign(t, lo, hi):
+            nc.vector.tensor_scalar(signed[:, t, lo:hi], larger[:, t, lo:hi], sign[:, t : t + 1], None, ALU.mult)
 
         def weave(half):
+            cols = slice(half * HALF, (half + 1) * HALF)
             nc.vector.tensor_copy(
-                woven[half][:].rearrange("p (c i) t -> p c t i", i=4),
-                signed[half][:].rearrange("p t (c i) -> p c t i", i=4),
+                woven[:, cols, :].rearrange("p (c i) t -> p c t i", i=4),
+                signed[:, :, cols].rearrange("p t (c i) -> p c t i", i=4),
             )
 
         def third_product(half):
-            z_codes = sb.tile([P, HALF], U32, name=f"z_codes{half}", align_bytes=64)
-            z_plane = sb.tile([P, HALF], U8, name=f"z_plane{half}", align_bytes=64)
+            cols = slice(half * HALF, (half + 1) * HALF)
             nc.vector.quantize_mx(
-                out=z_codes[:].bitcast(FP8X4), scales=z_plane[:], in_=woven[half][:].rearrange("p c t -> p (c t)")
+                out=z_codes[:, cols].bitcast(FP8X4),
+                scales=z_planes[half][:],
+                in_=woven[:, cols, :].rearrange("p c t -> p (c t)"),
             )
             for t in range(PACK):
-                product(h_ps[t][:, half * HALF : (half + 1) * HALF], w3, t, z_codes[:], z_plane[:])
+                product(h_ps[t][:, cols], w3_dealt, w3_plane[:], t, z_codes[:, cols], z_planes[half][:])
 
-        units = [(half, t) for half in range(2) for t in range(PACK)]
-        for u, (half, t) in enumerate(units):
-            ya, yb = fetch_y(half, t)
-            add_d(half, t, "a", ya, n3_t, False)
+        units = [(t, 0, S) for t in range(PACK - 1)] + [(PACK - 1, 0, HALF), (PACK - 1, HALF, S)]
+        for u, (t, lo, hi) in enumerate(units):
+            if lo == 0:
+                leave_psum(y[t], y_ps[t], t, False)
+            ya = fetch(y[t], n1_t, lo, hi, f"ya{t}_{lo}")
+            yb = fetch(y[t], n2_t, lo, hi, f"yb{t}_{lo}")
+            if lo == 0:
+                leave_psum(d[t], d_ps[t], t, t < 2)
+            add_d(t, lo, hi, "a", ya, n3_t, u == 4)
             if u > 0:
                 take_larger(*units[u - 1])
-            if u == PACK + 1:
-                third_product(0)
-            add_d(half, t, "b", yb, n4_t, t % 2 == 1)
+            add_d(t, lo, hi, "b", yb, n4_t, u >= 2)
             if u > 0:
                 apply_sign(*units[u - 1])
-            if u == 1:
-                w3.append(deal_words(w3w, "w3_dealt"))
-            if u == 2:
-                w3.append(deal_scales(nc.sync, w3s, 1, "w3_plane")[:])
-            if u == PACK:
-                weave(0)
-            if u >= PACK + 2:
-                for tt in (2 * (u - PACK - 2), 2 * (u - PACK - 2) + 1):
-                    nc.scalar.copy(h[tt][:, 0:HALF], h_ps[tt][:, 0:HALF])
+        weave(0)
         take_larger(*units[-1])
+        third_product(0)
         apply_sign(*units[-1])
+        for t in range(PACK):
+            nc.scalar.copy(h[t][:, 0:HALF], h_ps[t][:, 0:HALF])
         weave(1)
         third_product(1)
 
@@ -225,6 +223,7 @@ def tile_picked_twhpathbpolar_none_po_kernel(
         total = [sb.tile([P, W], F32, name=f"total{t}") for t in range(PACK)]
         root = [sb.tile([P, W], F32, name=f"root{t}") for t in range(PACK)]
         result = [sb.tile([P, S], F32, name=f"result{t}") for t in range(PACK)]
+        staged = sb.tile([P, PACK - 1, S], BF16, name="staged")
 
         def fetch_pair(t):
             if t < 2:
@@ -232,19 +231,27 @@ def tile_picked_twhpathbpolar_none_po_kernel(
             else:
                 nc.scalar.copy(h[t][:, HALF:S], h_ps[t][:, HALF:S])
             nc.scalar.activation(pair[t][:, 0, :], h[t][:].indirect(n5_t[:]), ACT.Copy, scale=-0.5)
-            if t < 2:
+            if t < 1:
                 nc.vector.tensor_copy(pair[t][:, 1, :], h[t][:].indirect(n6_t[:]))
             else:
                 nc.scalar.activation(pair[t][:, 1, :], h[t][:].indirect(n6_t[:]), ACT.Copy)
 
         def round_out(t):
-            nc.vector.tensor_copy(rounded[:, :, t], result[t][:])
+            if t == PACK - 1:
+                nc.vector.tensor_copy(rounded[:, :, t], result[t][:])
+                return
+            nc.vector.tensor_copy(staged[:, t, :], result[t][:])
+            if t == PACK - 2:
+                nc.vector.tensor_copy(rounded[:, :, 0 : PACK - 1], staged[:].rearrange("p t c -> p c t"))
 
         fetch_pair(0)
         for t in range(PACK):
             if t + 1 < PACK:
                 fetch_pair(t + 1)
-            nc.vector.tensor_tensor(squares[t][:], pair[t][:], pair[t][:], ALU.mult)
+            if True:
+                nc.vector.tensor_tensor(squares[t][:], pair[t][:], pair[t][:], ALU.mult)
+            else:
+                nc.scalar.activation(squares[t][:], pair[t][:], ACT.Square)
             if t > 1:
                 round_out(t - 2)
             nc.vector.scalar_tensor_tensor(total[t][:], squares[t][:, 0, :], 4.0, squares[t][:, 1, :], ALU.mult, ALU.add)

@@ -112,6 +112,8 @@ def tile_picked_twhpathbpolar_none_po_kernel(
         nc.gpsimd.tensor_tensor(size[:], gain[:], sign[:], ALU.mult)
         quarter = sb.tile([P, 1], F32, name="quarter")
         nc.gpsimd.memset(quarter[:], 0.25)
+        warm = sb.tile([P, 1], F32, name="warm")
+        nc.scalar.activation(warm[:], quarter[:], ACT.Sqrt)
 
         y = [sb.tile([P, 2 * S], F32, name=f"y{t}") for t in range(PACK)]
         d = [sb.tile([P, 2 * S], F32, name=f"d{t}") for t in range(PACK)]

@@ -115,14 +115,15 @@ def tile_picked_twhpathbpolar_none_po_kernel(
         warm = sb.tile([P, 1], F32, name="warm")
         nc.scalar.activation(warm[:], quarter[:], ACT.Sqrt)
 
-        y = [sb.tile([P, 2 * S], F32, name=f"y{t}") for t in range(PACK)]
-        d = [sb.tile([P, 2 * S], F32, name=f"d{t}") for t in range(PACK)]
+        LAST = PACK - 1
+        y = [sb.tile([P, S if t == LAST else 2 * S], F32, name=f"y{t}") for t in range(PACK)]
+        d = [sb.tile([P, S if t == LAST else 2 * S], F32, name=f"d{t}") for t in range(PACK)]
 
         w12_planes = deal_scales(nc.scalar, w12s, 2, "w12_planes")
+        w2w = load_words(nc.sync, w2_words, "w2w", "raw_scales")
         offs_plane = gather_plane(offs_t, "offs")
         hz_plane = gather_plane(hz_t, "hz")
         w1_dealt = deal_words(w1w, "w1_dealt")
-        w2w = load_words(nc.sync, w2_words, "w2w", "raw_words")
         offs_codes = sb.tile([P, S], U32, name="offs_codes", align_bytes=64)
         nc.vector.tensor_copy(offs_codes[:], xw[:].bitcast(U32).indirect(offs_t[:]))
         y_ps = [psum.tile([P, S], F32, name=f"y_ps{t}", tag=f"bank{t}") for t in range(PACK)]
@@ -134,19 +135,22 @@ def tile_picked_twhpathbpolar_none_po_kernel(
         d_ps = [psum.tile([P, S], F32, name=f"d_ps{t}", tag=f"bank{PACK + t}") for t in range(PACK)]
         for t in range(PACK):
             product(d_ps[t][:], w2_dealt, w12_planes[:, H : 2 * H], t, hz_codes[:], hz_plane[:])
-        w3s = sb.tile([P, H], U8, name="w3s", tag="raw_scales", align_bytes=64)
+        w3s = sb.tile([P, H], U8, name="w3s", tag="raw_words", align_bytes=64)
         load_scale_rows(nc.sync, w3_scales, w3s[:])
-        w3w = load_words(nc.sync, w3_words, "w3w", "raw_words")
+        w3w = load_words(nc.sync, w3_words, "w3w", "raw_scales")
         w3_plane = deal_scales(nc.sync, w3s, 1, "w3_plane")
         w3_dealt = deal_words(w3w, "w3_dealt")
 
         h = [sb.tile([P, S], F32, name=f"h{t}") for t in range(PACK)]
-        h_ps = [psum.tile([P, S], F32, name=f"h_ps{t}", tag=f"bank{t}") for t in range(PACK)]
+        h_ps = [
+            [psum.tile([P, HALF], F32, name=f"h_ps{half}{t}", tag=f"bank{PACK * half + t}") for t in range(PACK)]
+            for half in range(2)
+        ]
         larger = sb.tile([P, PACK, S], BF16, name="larger")
         signed = sb.tile([P, PACK, S], BF16, name="signed")
         woven = sb.tile([P, S, PACK], BF16, name="woven", align_bytes=64)
         z_codes = sb.tile([P, S], U32, name="z_codes", align_bytes=64)
-        z_planes = [sb.tile([P, HALF], U8, name=f"z_plane{half}", align_bytes=64) for half in range(2)]
+        z_plane = sb.tile([P, S], U8, name="z_plane", align_bytes=64)
         sums = {}
 
         def entries(offsets, lo, hi):
@@ -178,45 +182,64 @@ def tile_picked_twhpathbpolar_none_po_kernel(
         def apply_sign(t, lo, hi):
             nc.vector.tensor_scalar(signed[:, t, lo:hi], larger[:, t, lo:hi], sign[:, t : t + 1], None, ALU.mult)
 
-        def weave(half):
-            cols = slice(half * HALF, (half + 1) * HALF)
+        def weave(lo, hi):
             nc.vector.tensor_copy(
-                woven[:, cols, :].rearrange("p (c i) t -> p c t i", i=4),
-                signed[:, :, cols].rearrange("p t (c i) -> p c t i", i=4),
+                woven[:, lo:hi, :].rearrange("p (c i) t -> p c t i", i=4),
+                signed[:, :, lo:hi].rearrange("p t (c i) -> p c t i", i=4),
             )
 
-        def third_product(half):
-            cols = slice(half * HALF, (half + 1) * HALF)
+        def third_product(lo, hi):
             nc.vector.quantize_mx(
-                out=z_codes[:, cols].bitcast(FP8X4),
-                scales=z_planes[half][:],
-                in_=woven[:, cols, :].rearrange("p c t -> p (c t)"),
+                out=z_codes[:, lo:hi].bitcast(FP8X4),
+                scales=z_plane[:, lo:hi],
+                in_=woven[:, lo:hi, :].rearrange("p c t -> p (c t)"),
             )
             for t in range(PACK):
-                product(h_ps[t][:, cols], w3_dealt, w3_plane[:], t, z_codes[:, cols], z_planes[half][:])
+                product(h_ps[lo // HALF][t][:, lo % HALF : lo % HALF + hi - lo], w3_dealt, w3_plane[:], t, z_codes[:, lo:hi], z_plane[:, lo:hi])
 
-        units = [(t, 0, S) for t in range(PACK - 1)] + [(PACK - 1, 0, HALF), (PACK - 1, HALF, S)]
-        for u, (t, lo, hi) in enumerate(units):
-            if lo == 0:
-                leave_psum(y[t], y_ps[t], t, False)
-            ya = fetch(y[t], n1_t, lo, hi, f"ya{t}_{lo}")
-            yb = fetch(y[t], n2_t, lo, hi, f"yb{t}_{lo}")
-            if lo == 0:
-                leave_psum(d[t], d_ps[t], t, t < 2)
-            add_d(t, lo, hi, "a", ya, n3_t, u == 4)
-            if u > 0:
-                take_larger(*units[u - 1])
-            add_d(t, lo, hi, "b", yb, n4_t, u >= 2)
-            if u > 0:
-                apply_sign(*units[u - 1])
-        weave(0)
-        take_larger(*units[-1])
-        third_product(0)
-        apply_sign(*units[-1])
-        for t in range(PACK):
-            nc.scalar.copy(h[t][:, 0:HALF], h_ps[t][:, 0:HALF])
-        weave(1)
-        third_product(1)
+        for t in range(LAST):
+            leave_psum(y[t], y_ps[t], t, False)
+            ya = fetch(y[t], n1_t, 0, S, f"ya{t}")
+            yb = fetch(y[t], n2_t, 0, S, f"yb{t}")
+            leave_psum(d[t], d_ps[t], t, t < 2)
+            add_d(t, 0, S, "a", ya, n3_t, False)
+            if t > 0:
+                take_larger(t - 1, 0, S)
+            add_d(t, 0, S, "b", yb, n4_t, t == LAST - 1)
+            if t > 0:
+                apply_sign(t - 1, 0, S)
+        t = LAST
+        leave_psum(y[t], y_ps[t], t, False)
+        leave_psum(d[t], d_ps[t], t, t < 2)
+        first, second, third = (0, HALF), (HALF, HALF + HALF // 2), (HALF + HALF // 2, S)
+        ya = fetch(y[t], n1_t, *first, "ya_first")
+        add_d(t, *first, "a", ya, n3_t, False)
+        take_larger(t - 1, 0, S)
+        yb = fetch(y[t], n2_t, *first, "yb_first")
+        add_d(t, *first, "b", yb, n4_t, True)
+        apply_sign(t - 1, 0, S)
+        take_larger(t, *first)
+        ya = fetch(y[t], n1_t, *second, "ya_second")
+        add_d(t, *second, "a", ya, n3_t, False)
+        apply_sign(t, *first)
+        yb = fetch(y[t], n2_t, *second, "yb_second")
+        add_d(t, *second, "b", yb, n4_t, True)
+        weave(*first)
+        take_larger(t, *second)
+        third_product(*first)
+        apply_sign(t, *second)
+        ya = fetch(y[t], n1_t, *third, "ya_third")
+        add_d(t, *third, "a", ya, n3_t, True)
+        weave(*second)
+        yb = fetch(y[t], n2_t, *third, "yb_third")
+        add_d(t, *third, "b", yb, n4_t, True)
+        third_product(*second)
+        take_larger(t, *third)
+        apply_sign(t, *third)
+        for u in range(PACK):
+            nc.scalar.copy(h[u][:, 0:HALF], h_ps[0][u][:])
+        weave(*third)
+        third_product(*third)
 
         out_rows = out_0.rearrange("(p t) c -> p t c", t=PACK)
         rounded = sb.tile([P, S, PACK], BF16, name="rounded", align_bytes=64)
@@ -229,9 +252,9 @@ def tile_picked_twhpathbpolar_none_po_kernel(
 
         def fetch_pair(t):
             if t < 2:
-                nc.vector.tensor_copy(h[t][:, HALF:S], h_ps[t][:, HALF:S])
+                nc.vector.tensor_copy(h[t][:, HALF:S], h_ps[1][t][:])
             else:
-                nc.scalar.copy(h[t][:, HALF:S], h_ps[t][:, HALF:S])
+                nc.scalar.copy(h[t][:, HALF:S], h_ps[1][t][:])
             nc.scalar.activation(pair[t][:, 0, :], h[t][:].indirect(n5_t[:]), ACT.Copy, scale=-0.5)
             if t < 1:
                 nc.vector.tensor_copy(pair[t][:, 1, :], h[t][:].indirect(n6_t[:]))
@@ -246,30 +269,41 @@ def tile_picked_twhpathbpolar_none_po_kernel(
             if t == PACK - 2:
                 nc.vector.tensor_copy(rounded[:, :, 0 : PACK - 1], staged[:].rearrange("p t c -> p c t"))
 
-        fetch_pair(0)
-        for t in range(PACK):
-            if t + 1 < PACK:
-                fetch_pair(t + 1)
-            if True:
-                nc.vector.tensor_tensor(squares[t][:], pair[t][:], pair[t][:], ALU.mult)
-            else:
-                nc.scalar.activation(squares[t][:], pair[t][:], ACT.Square)
-            if t > 1:
-                round_out(t - 2)
+        def square(t):
+            nc.vector.tensor_tensor(squares[t][:], pair[t][:], pair[t][:], ALU.mult)
+
+        def add_squares(t):
             nc.vector.scalar_tensor_tensor(total[t][:], squares[t][:, 0, :], 4.0, squares[t][:, 1, :], ALU.mult, ALU.add)
+
+        for t in range(PACK - 1):
+            fetch_pair(t)
+        square(0)
+        for t in range(PACK):
+            add_squares(t)
+            if t + 1 < PACK:
+                square(t + 1)
             nc.vector.tensor_tensor(result[t][:].indirect(n6_t[:]), pair[t][:, 1, :], pair[t][:, 0, :], ALU.add)
             nc.scalar.activation(root[t][:], total[t][:], ACT.Sqrt, bias=quarter[:])
             nc.scalar.activation(result[t][:].indirect(n5_t[:]), root[t][:], ACT.Copy)
             nc.sync.dma_start(out_rows[:, t, :], result[t][:])
-        round_out(PACK - 2)
-        round_out(PACK - 1)
+            if t == 0:
+                fetch_pair(PACK - 1)
+        for t in range(LAST):
+            round_out(t)
 
         out_codes = sb.tile([P, S], I32, name="out_codes", align_bytes=64)
         out_plane = sb.tile([P, S], U8, name="out_plane", align_bytes=64)
-        nc.vector.quantize_mx(
-            out=out_codes[:].bitcast(FP8X4), scales=out_plane[:], in_=rounded[:].rearrange("p c t -> p (c t)")
-        )
-        nc.sync.dma_start(out_1[0].rearrange("p c r -> p (c r)").bitcast(I32), out_codes[:])
+        out_words = out_1[0].rearrange("p c r -> p (c r)").bitcast(I32)
+        halves = [slice(0, HALF), slice(HALF, S)]
+        for cols in halves:
+            nc.vector.tensor_copy(rounded[:, cols, LAST], result[LAST][:, cols])
+        for cols in halves:
+            nc.vector.quantize_mx(
+                out=out_codes[:, cols].bitcast(FP8X4),
+                scales=out_plane[:, cols],
+                in_=rounded[:, cols, :].rearrange("p c t -> p (c t)"),
+            )
+            nc.sync.dma_start(out_words[:, cols], out_codes[:, cols])
         for q in range(4):
             queue = nc.scalar if q % 2 == 0 else nc.sync
             queue.dma_start(out_2[0, 4 * q : 4 * q + 4, :].bitcast(I32), out_plane[32 * q : 32 * q + 4, :].bitcast(I32))

@@ -2,7 +2,7 @@ from contextlib import ExitStack
 
 import concourse.mybir as mybir
 
-K, T, S, H, N, W = 512, 2048, 512, 512, 512, 256
+T, S, H, W = 2048, 512, 512, 256
 FLOPS = 3 * 2 * 512 * 512 * 512
 
 F32 = mybir.dt.float32
@@ -18,7 +18,12 @@ ACT = mybir.ActivationFunctionType
 
 P = 128
 PACK = 4
+LAST = PACK - 1
 HALF = S // 2
+BLOCKS = 16
+BLOCK_PARTITIONS = P // BLOCKS
+QUADRANT = 32
+FIRST, SECOND, THIRD = (0, HALF), (HALF, HALF + HALF // 2), (HALF + HALF // 2, S)
 
 
 def tile_picked_twhpathbpolar_none_po_kernel(
@@ -38,11 +43,13 @@ def tile_picked_twhpathbpolar_none_po_kernel(
 
         def load_scale_rows(queue, src, dst):
             rows = src[0].bitcast(I32)
-            queue.dma_start(dst.bitcast(I32), rows.unsqueeze(1).to_broadcast([16, 8, rows.shape[1]]))
+            queue.dma_start(dst.bitcast(I32), rows.unsqueeze(1).to_broadcast([BLOCKS, BLOCK_PARTITIONS, rows.shape[1]]))
 
         def place_scale_rows(queue, plane, spread):
             for r in range(1, 4):
-                queue.dma_start(plane[r:P:32, :].bitcast(I32), spread[8 * r : P : 32, :].bitcast(I32))
+                queue.dma_start(
+                    plane[r:P:QUADRANT, :].bitcast(I32), spread[BLOCK_PARTITIONS * r : P : QUADRANT, :].bitcast(I32)
+                )
 
         def load_words(queue, src, name, tag):
             tile = sb.tile([P, 2 * H], U8, name=name, tag=tag, align_bytes=64)
@@ -68,7 +75,7 @@ def tile_picked_twhpathbpolar_none_po_kernel(
 
         def gather_plane(offsets, name):
             picked = sb.tile([P, S], U8, name=name + "_bytes", align_bytes=64)
-            nc.vector.tensor_copy(picked[:], xs[:].indirect(offsets[:]))
+            nc.vector.tensor_copy(picked[:], x_rows[:].indirect(offsets[:]))
             plane = sb.tile([P, S], U8, name=name + "_plane", align_bytes=64)
             nc.vector.tensor_copy(plane[:].bitcast(I32), picked[:].bitcast(I32))
             place_scale_rows(nc.sync, plane, picked)
@@ -85,61 +92,64 @@ def tile_picked_twhpathbpolar_none_po_kernel(
                 stop=True,
             )
 
-        xs = sb.tile([P, T], U8, name="xs", align_bytes=64)
-        load_scale_rows(nc.sync, x_scales, xs[:])
-        w12s = sb.tile([P, 2 * H], U8, name="w12s", tag="raw_scales", align_bytes=64)
-        load_scale_rows(nc.scalar, w1_scales, w12s[:, 0:H])
-        offs_t = load_list(offs, "offs_t")
-        load_scale_rows(nc.scalar, w2_scales, w12s[:, H : 2 * H])
-        hz_t = load_list(hz, "hz_t")
-        w1w = load_words(nc.scalar, w1_words, "w1w", "raw_words")
-        n1_t = load_list(n1, "n1_t")
-        xw = sb.tile([P, T], I32, name="xw", align_bytes=64)
-        nc.sync.dma_start(xw[:], x_words[0].rearrange("p c r -> p (c r)").bitcast(I32))
+        w12_rows = sb.tile([P, 2 * H], U8, name="w12_rows", tag="raw_a", align_bytes=64)
+        load_scale_rows(nc.sync, w2_scales, w12_rows[:, H : 2 * H])
+        load_scale_rows(nc.scalar, w1_scales, w12_rows[:, 0:H])
+        offs_list = load_list(offs, "offs_list")
+        x_rows = sb.tile([P, T], U8, name="x_rows", align_bytes=64)
+        load_scale_rows(nc.scalar, x_scales, x_rows[:])
+        hz_list = load_list(hz, "hz_list")
+        w1_raw = load_words(nc.sync, w1_words, "w1_raw", "raw_b")
+        n1_list = load_list(n1, "n1_list")
+        x_table = sb.tile([P, T], I32, name="x_table", align_bytes=64)
+        nc.sync.dma_start(x_table[:], x_words[0].rearrange("p c r -> p (c r)").bitcast(I32))
         gain = sb.tile([P, PACK], F32, name="gain")
         nc.gpsimd.dma_start(gain[:], gn.rearrange("(p t) o -> p (t o)", t=PACK))
-        n2_t = load_list(n2, "n2_t")
-        n3_t = load_list(n3, "n3_t")
-        n4_t = load_list(n4, "n4_t")
-        n5_t = load_list(n5, "n5_t")
-        n6_t = load_list(n6, "n6_t")
+        n2_list = load_list(n2, "n2_list")
+        n3_list = load_list(n3, "n3_list")
+        n4_list = load_list(n4, "n4_list")
+        n5_list = load_list(n5, "n5_list")
+        n6_list = load_list(n6, "n6_list")
 
         sign = sb.tile([P, PACK], F32, name="sign")
-        step = sb.tile([P, PACK], F32, name="step")
+        twice_nonnegative = sb.tile([P, PACK], F32, name="twice_nonnegative")
         size = sb.tile([P, PACK], F32, name="size")
-        nc.gpsimd.tensor_scalar(step[:], gain[:], 0.0, 2.0, ALU.is_ge, ALU.mult)
-        nc.gpsimd.tensor_scalar(sign[:], step[:], 1.0, -1.0, ALU.mult, ALU.add)
+        nc.gpsimd.tensor_scalar(twice_nonnegative[:], gain[:], 0.0, 2.0, ALU.is_ge, ALU.mult)
+        nc.gpsimd.tensor_scalar(sign[:], twice_nonnegative[:], 1.0, -1.0, ALU.mult, ALU.add)
         nc.gpsimd.tensor_tensor(size[:], gain[:], sign[:], ALU.mult)
         quarter = sb.tile([P, 1], F32, name="quarter")
         nc.gpsimd.memset(quarter[:], 0.25)
         warm = sb.tile([P, 1], F32, name="warm")
         nc.scalar.activation(warm[:], quarter[:], ACT.Sqrt)
 
-        LAST = PACK - 1
         y = [sb.tile([P, S if t == LAST else 2 * S], F32, name=f"y{t}") for t in range(PACK)]
         d = [sb.tile([P, S if t == LAST else 2 * S], F32, name=f"d{t}") for t in range(PACK)]
 
-        w12_planes = deal_scales(nc.scalar, w12s, 2, "w12_planes")
-        w2w = load_words(nc.sync, w2_words, "w2w", "raw_scales")
-        offs_plane = gather_plane(offs_t, "offs")
-        hz_plane = gather_plane(hz_t, "hz")
-        w1_dealt = deal_words(w1w, "w1_dealt")
+        w12_planes = deal_scales(nc.scalar, w12_rows, 2, "w12_planes")
+        w1_plane, w2_plane = w12_planes[:, 0:H], w12_planes[:, H : 2 * H]
+        w2_raw = load_words(nc.sync, w2_words, "w2_raw", "raw_a")
+        offs_plane = gather_plane(offs_list, "offs")
+        hz_plane = gather_plane(hz_list, "hz")
+        w1_dealt = deal_words(w1_raw, "w1_dealt")
         offs_codes = sb.tile([P, S], U32, name="offs_codes", align_bytes=64)
-        nc.vector.tensor_copy(offs_codes[:], xw[:].bitcast(U32).indirect(offs_t[:]))
+        nc.vector.tensor_copy(offs_codes[:], x_table[:].bitcast(U32).indirect(offs_list[:]))
         y_ps = [psum.tile([P, S], F32, name=f"y_ps{t}", tag=f"bank{t}") for t in range(PACK)]
-        for t in range(PACK):
-            product(y_ps[t][:], w1_dealt, w12_planes[:, 0:H], t, offs_codes[:], offs_plane[:])
-        w2_dealt = deal_words(w2w, "w2_dealt")
+        lead = 2
+        for t in range(lead):
+            product(y_ps[t][:], w1_dealt, w1_plane, t, offs_codes[:], offs_plane[:])
+        w2_dealt = deal_words(w2_raw, "w2_dealt")
         hz_codes = sb.tile([P, S], U32, name="hz_codes", align_bytes=64)
-        nc.vector.tensor_copy(hz_codes[:], xw[:].bitcast(U32).indirect(hz_t[:]))
+        nc.vector.tensor_copy(hz_codes[:], x_table[:].bitcast(U32).indirect(hz_list[:]))
         d_ps = [psum.tile([P, S], F32, name=f"d_ps{t}", tag=f"bank{PACK + t}") for t in range(PACK)]
         for t in range(PACK):
-            product(d_ps[t][:], w2_dealt, w12_planes[:, H : 2 * H], t, hz_codes[:], hz_plane[:])
-        w3s = sb.tile([P, H], U8, name="w3s", tag="raw_words", align_bytes=64)
-        load_scale_rows(nc.sync, w3_scales, w3s[:])
-        w3w = load_words(nc.sync, w3_words, "w3w", "raw_scales")
-        w3_plane = deal_scales(nc.sync, w3s, 1, "w3_plane")
-        w3_dealt = deal_words(w3w, "w3_dealt")
+            product(d_ps[t][:], w2_dealt, w2_plane, t, hz_codes[:], hz_plane[:])
+            if t + lead < PACK:
+                product(y_ps[t + lead][:], w1_dealt, w1_plane, t + lead, offs_codes[:], offs_plane[:])
+        w3_rows = sb.tile([P, H], U8, name="w3_rows", tag="raw_b", align_bytes=64)
+        load_scale_rows(nc.sync, w3_scales, w3_rows[:])
+        w3_raw = load_words(nc.sync, w3_words, "w3_raw", "raw_a")
+        w3_plane = deal_scales(nc.sync, w3_rows, 1, "w3_plane")
+        w3_dealt = deal_words(w3_raw, "w3_dealt")
 
         h = [sb.tile([P, S], F32, name=f"h{t}") for t in range(PACK)]
         h_ps = [
@@ -167,9 +177,9 @@ def tile_picked_twhpathbpolar_none_po_kernel(
             nc.scalar.activation(fetched[:], window[:].indirect(entries(offsets, lo, hi)), ACT.Copy)
             return fetched
 
-        def add_d(t, lo, hi, which, looked_up, offsets, on_scalar):
+        def add_d(t, lo, hi, which, looked_up, offsets, fetch_on_scalar):
             total = sb.tile([P, hi - lo], F32, name=f"sum{which}{t}_{lo}")
-            if on_scalar:
+            if fetch_on_scalar:
                 fetched = fetch(d[t], offsets, lo, hi, f"d{which}{t}_{lo}")
                 nc.vector.tensor_tensor(total[:], fetched[:], looked_up[:], ALU.add)
             else:
@@ -195,102 +205,100 @@ def tile_picked_twhpathbpolar_none_po_kernel(
                 in_=woven[:, lo:hi, :].rearrange("p c t -> p (c t)"),
             )
             for t in range(PACK):
-                product(h_ps[lo // HALF][t][:, lo % HALF : lo % HALF + hi - lo], w3_dealt, w3_plane[:], t, z_codes[:, lo:hi], z_plane[:, lo:hi])
+                out = h_ps[lo // HALF][t][:, lo % HALF : lo % HALF + hi - lo]
+                product(out, w3_dealt, w3_plane[:], t, z_codes[:, lo:hi], z_plane[:, lo:hi])
 
         for t in range(LAST):
-            leave_psum(y[t], y_ps[t], t, False)
-            ya = fetch(y[t], n1_t, 0, S, f"ya{t}")
-            yb = fetch(y[t], n2_t, 0, S, f"yb{t}")
-            leave_psum(d[t], d_ps[t], t, t < 2)
-            add_d(t, 0, S, "a", ya, n3_t, False)
+            leave_psum(y[t], y_ps[t], t, t == 1)
+            ya = fetch(y[t], n1_list, 0, S, f"ya{t}")
+            yb = fetch(y[t], n2_list, 0, S, f"yb{t}")
+            leave_psum(d[t], d_ps[t], t, t == 0)
+            add_d(t, 0, S, "a", ya, n3_list, False)
             if t > 0:
                 take_larger(t - 1, 0, S)
-            add_d(t, 0, S, "b", yb, n4_t, t == LAST - 1)
+            add_d(t, 0, S, "b", yb, n4_list, t == LAST - 1)
             if t > 0:
                 apply_sign(t - 1, 0, S)
-        t = LAST
-        leave_psum(y[t], y_ps[t], t, False)
-        leave_psum(d[t], d_ps[t], t, t < 2)
-        first, second, third = (0, HALF), (HALF, HALF + HALF // 2), (HALF + HALF // 2, S)
-        ya = fetch(y[t], n1_t, *first, "ya_first")
-        add_d(t, *first, "a", ya, n3_t, False)
-        take_larger(t - 1, 0, S)
-        yb = fetch(y[t], n2_t, *first, "yb_first")
-        add_d(t, *first, "b", yb, n4_t, True)
-        apply_sign(t - 1, 0, S)
-        take_larger(t, *first)
-        ya = fetch(y[t], n1_t, *second, "ya_second")
-        add_d(t, *second, "a", ya, n3_t, False)
-        apply_sign(t, *first)
-        yb = fetch(y[t], n2_t, *second, "yb_second")
-        add_d(t, *second, "b", yb, n4_t, True)
-        weave(*first)
-        take_larger(t, *second)
-        third_product(*first)
-        apply_sign(t, *second)
-        ya = fetch(y[t], n1_t, *third, "ya_third")
-        add_d(t, *third, "a", ya, n3_t, True)
-        weave(*second)
-        yb = fetch(y[t], n2_t, *third, "yb_third")
-        add_d(t, *third, "b", yb, n4_t, True)
-        third_product(*second)
-        take_larger(t, *third)
-        apply_sign(t, *third)
-        for u in range(PACK):
-            nc.scalar.copy(h[u][:, 0:HALF], h_ps[0][u][:])
-        weave(*third)
-        third_product(*third)
+        leave_psum(y[LAST], y_ps[LAST], LAST, False)
+        leave_psum(d[LAST], d_ps[LAST], LAST, False)
+        ya = fetch(y[LAST], n1_list, *FIRST, "ya_first")
+        add_d(LAST, *FIRST, "a", ya, n3_list, False)
+        take_larger(LAST - 1, 0, S)
+        yb = fetch(y[LAST], n2_list, *FIRST, "yb_first")
+        add_d(LAST, *FIRST, "b", yb, n4_list, True)
+        apply_sign(LAST - 1, 0, S)
+        take_larger(LAST, *FIRST)
+        ya = fetch(y[LAST], n1_list, *SECOND, "ya_second")
+        add_d(LAST, *SECOND, "a", ya, n3_list, False)
+        apply_sign(LAST, *FIRST)
+        yb = fetch(y[LAST], n2_list, *SECOND, "yb_second")
+        add_d(LAST, *SECOND, "b", yb, n4_list, True)
+        weave(*FIRST)
+        take_larger(LAST, *SECOND)
+        third_product(*FIRST)
+        apply_sign(LAST, *SECOND)
+        ya = fetch(y[LAST], n1_list, *THIRD, "ya_third")
+        add_d(LAST, *THIRD, "a", ya, n3_list, True)
+        weave(*SECOND)
+        yb = fetch(y[LAST], n2_list, *THIRD, "yb_third")
+        add_d(LAST, *THIRD, "b", yb, n4_list, True)
+        third_product(*SECOND)
+        take_larger(LAST, *THIRD)
+        apply_sign(LAST, *THIRD)
+        for t in range(PACK):
+            nc.scalar.copy(h[t][:, 0:HALF], h_ps[0][t][:])
+        weave(*THIRD)
+        third_product(*THIRD)
 
         out_rows = out_0.rearrange("(p t) c -> p t c", t=PACK)
         rounded = sb.tile([P, S, PACK], BF16, name="rounded", align_bytes=64)
         pair = [sb.tile([P, 2, W], F32, name=f"pair{t}") for t in range(PACK)]
         squares = [sb.tile([P, 2, W], F32, name=f"squares{t}") for t in range(PACK)]
-        total = [sb.tile([P, W], F32, name=f"total{t}") for t in range(PACK)]
+        radicand = [sb.tile([P, W], F32, name=f"radicand{t}") for t in range(PACK)]
         root = [sb.tile([P, W], F32, name=f"root{t}") for t in range(PACK)]
         result = [sb.tile([P, S], F32, name=f"result{t}") for t in range(PACK)]
-        staged = sb.tile([P, PACK - 1, S], BF16, name="staged")
+        staged = sb.tile([P, LAST, S], BF16, name="staged")
 
-        def fetch_pair(t):
-            if t < 2:
+        def finish_h(t):
+            if t < LAST:
                 nc.vector.tensor_copy(h[t][:, HALF:S], h_ps[1][t][:])
             else:
                 nc.scalar.copy(h[t][:, HALF:S], h_ps[1][t][:])
-            nc.scalar.activation(pair[t][:, 0, :], h[t][:].indirect(n5_t[:]), ACT.Copy, scale=-0.5)
-            if t < 1:
-                nc.vector.tensor_copy(pair[t][:, 1, :], h[t][:].indirect(n6_t[:]))
-            else:
-                nc.scalar.activation(pair[t][:, 1, :], h[t][:].indirect(n6_t[:]), ACT.Copy)
 
-        def round_out(t):
-            if t == PACK - 1:
-                nc.vector.tensor_copy(rounded[:, :, t], result[t][:])
-                return
-            nc.vector.tensor_copy(staged[:, t, :], result[t][:])
-            if t == PACK - 2:
-                nc.vector.tensor_copy(rounded[:, :, 0 : PACK - 1], staged[:].rearrange("p t c -> p c t"))
+        def fetch_pair(t):
+            nc.scalar.activation(pair[t][:, 0, :], h[t][:].indirect(n5_list[:]), ACT.Copy, scale=-0.5)
+            if t == 0:
+                nc.vector.tensor_copy(pair[t][:, 1, :], h[t][:].indirect(n6_list[:]))
+            else:
+                nc.scalar.activation(pair[t][:, 1, :], h[t][:].indirect(n6_list[:]), ACT.Copy)
 
         def square(t):
             nc.vector.tensor_tensor(squares[t][:], pair[t][:], pair[t][:], ALU.mult)
 
-        def add_squares(t):
-            nc.vector.scalar_tensor_tensor(total[t][:], squares[t][:, 0, :], 4.0, squares[t][:, 1, :], ALU.mult, ALU.add)
-
-        for t in range(PACK - 1):
-            fetch_pair(t)
+        finish_h(0)
+        finish_h(1)
+        fetch_pair(0)
+        fetch_pair(1)
         square(0)
+        finish_h(2)
+        fetch_pair(2)
         for t in range(PACK):
-            add_squares(t)
-            if t + 1 < PACK:
+            nc.vector.scalar_tensor_tensor(
+                radicand[t][:], squares[t][:, 0, :], 4.0, squares[t][:, 1, :], ALU.mult, ALU.add
+            )
+            if t < LAST:
                 square(t + 1)
-            nc.vector.tensor_tensor(result[t][:].indirect(n6_t[:]), pair[t][:, 1, :], pair[t][:, 0, :], ALU.add)
-            nc.scalar.activation(root[t][:], total[t][:], ACT.Sqrt, bias=quarter[:])
-            nc.scalar.activation(result[t][:].indirect(n5_t[:]), root[t][:], ACT.Copy)
+            nc.vector.tensor_tensor(result[t][:].indirect(n6_list[:]), pair[t][:, 1, :], pair[t][:, 0, :], ALU.add)
+            nc.scalar.activation(root[t][:], radicand[t][:], ACT.Sqrt, bias=quarter[:])
+            nc.scalar.activation(result[t][:].indirect(n5_list[:]), root[t][:], ACT.Copy)
             nc.sync.dma_start(out_rows[:, t, :], result[t][:])
             if t == 0:
-                fetch_pair(PACK - 1)
-        for t in range(LAST):
-            round_out(t)
+                finish_h(LAST)
+                fetch_pair(LAST)
 
+        for t in range(LAST):
+            nc.vector.tensor_copy(staged[:, t, :], result[t][:])
+        nc.vector.tensor_copy(rounded[:, :, 0:LAST], staged[:].rearrange("p t c -> p c t"))
         out_codes = sb.tile([P, S], I32, name="out_codes", align_bytes=64)
         out_plane = sb.tile([P, S], U8, name="out_plane", align_bytes=64)
         out_words = out_1[0].rearrange("p c r -> p (c r)").bitcast(I32)
@@ -306,4 +314,6 @@ def tile_picked_twhpathbpolar_none_po_kernel(
             nc.sync.dma_start(out_words[:, cols], out_codes[:, cols])
         for q in range(4):
             queue = nc.scalar if q % 2 == 0 else nc.sync
-            queue.dma_start(out_2[0, 4 * q : 4 * q + 4, :].bitcast(I32), out_plane[32 * q : 32 * q + 4, :].bitcast(I32))
+            queue.dma_start(
+                out_2[0, 4 * q : 4 * q + 4, :].bitcast(I32), out_plane[QUADRANT * q : QUADRANT * q + 4, :].bitcast(I32)
+            )

from contextlib import ExitStack

import concourse.mybir as mybir

T, S, H, W = 2048, 512, 512, 256
FLOPS = 3 * 2 * 512 * 512 * 512

F32 = mybir.dt.float32
BF16 = mybir.dt.bfloat16
I32 = mybir.dt.int32
U32 = mybir.dt.uint32
U16 = mybir.dt.uint16
U8 = mybir.dt.uint8
FP8X4 = mybir.dt.float8_e4m3fn_x4
FP4X4 = mybir.dt.float4_e2m1fn_x4
ALU = mybir.AluOpType
ACT = mybir.ActivationFunctionType

P = 128
PACK = 4
LAST = PACK - 1
HALF = S // 2
BLOCKS = 16
BLOCK_PARTITIONS = P // BLOCKS
QUADRANT = 32
FIRST, SECOND, THIRD = (0, HALF), (HALF, HALF + HALF // 2), (HALF + HALF // 2, S)


def tile_picked_twhpathbpolar_none_po_kernel(
    tc, x_words, x_scales, w1_words, w1_scales, w2_words, w2_scales, gn, w3_words, w3_scales,
    offs, hz, n1, n2, n3, n4, n5, n6, out_0, out_1, out_2,
):
    nc = tc.nc
    with ExitStack() as ctx:
        lists = ctx.enter_context(tc.tile_pool(name="lists", bufs=1))
        sb = ctx.enter_context(tc.tile_pool(name="sb", bufs=1))
        psum = ctx.enter_context(tc.psum_pool(name="psum", bufs=1))

        def load_list(src, name):
            tile = lists.tile(list(src.shape), U16, name=name)
            nc.sync.dma_start(tile[:], src)
            return tile

        def load_scale_rows(queue, src, dst):
            rows = src[0].bitcast(I32)
            queue.dma_start(dst.bitcast(I32), rows.unsqueeze(1).to_broadcast([BLOCKS, BLOCK_PARTITIONS, rows.shape[1]]))

        def place_scale_rows(queue, plane, spread):
            for r in range(1, 4):
                queue.dma_start(
                    plane[r:P:QUADRANT, :].bitcast(I32), spread[BLOCK_PARTITIONS * r : P : QUADRANT, :].bitcast(I32)
                )

        def load_words(queue, src, name, tag):
            tile = sb.tile([P, 2 * H], U8, name=name, tag=tag, align_bytes=64)
            queue.dma_start(tile[:].bitcast(I32), src[0].bitcast(I32))
            return tile

        def deal_scales(queue, scales, count, name):
            dealt = sb.tile([P, count * H], U8, name=name, align_bytes=64)
            nc.vector.tensor_copy(
                dealt[:].rearrange("p (w t m) -> p w t m", w=count, t=PACK),
                scales[:].rearrange("p (w m t) -> p w t m", w=count, t=PACK),
            )
            place_scale_rows(queue, dealt, dealt)
            return dealt

        def deal_words(words, name):
            dealt = sb.tile([P, 2 * H], U8, name=name, align_bytes=64)
            nc.vector.tensor_copy(
                dealt[:].rearrange("p (t m b) -> p t m b", t=PACK, b=2),
                words[:].rearrange("p (m t b) -> p t m b", t=PACK, b=2),
            )
            return dealt

        def gather_plane(offsets, name):
            picked = sb.tile([P, S], U8, name=name + "_bytes", align_bytes=64)
            nc.vector.tensor_copy(picked[:], x_rows[:].indirect(offsets[:]))
            plane = sb.tile([P, S], U8, name=name + "_plane", align_bytes=64)
            nc.vector.tensor_copy(plane[:].bitcast(I32), picked[:].bitcast(I32))
            place_scale_rows(nc.sync, plane, picked)
            return plane

        def product(out, words, plane, t, codes, scales):
            nc.tensor.matmul_mx(
                out=out,
                lhsT=words[:, 2 * P * t : 2 * P * (t + 1)].bitcast(FP4X4),
                lhsT_scale=plane[:, P * t : P * (t + 1)],
                rhs=codes.bitcast(FP8X4),
                rhs_scale=scales,
                start=True,
                stop=True,
            )

        w12_rows = sb.tile([P, 2 * H], U8, name="w12_rows", tag="raw_a", align_bytes=64)
        load_scale_rows(nc.sync, w2_scales, w12_rows[:, H : 2 * H])
        load_scale_rows(nc.scalar, w1_scales, w12_rows[:, 0:H])
        offs_list = load_list(offs, "offs_list")
        x_rows = sb.tile([P, T], U8, name="x_rows", align_bytes=64)
        load_scale_rows(nc.scalar, x_scales, x_rows[:])
        hz_list = load_list(hz, "hz_list")
        w1_raw = load_words(nc.sync, w1_words, "w1_raw", "raw_b")
        n1_list = load_list(n1, "n1_list")
        x_table = sb.tile([P, T], I32, name="x_table", align_bytes=64)
        nc.sync.dma_start(x_table[:], x_words[0].rearrange("p c r -> p (c r)").bitcast(I32))
        gain = sb.tile([P, PACK], F32, name="gain")
        nc.gpsimd.dma_start(gain[:], gn.rearrange("(p t) o -> p (t o)", t=PACK))
        n2_list = load_list(n2, "n2_list")
        n3_list = load_list(n3, "n3_list")
        n4_list = load_list(n4, "n4_list")
        n5_list = load_list(n5, "n5_list")
        n6_list = load_list(n6, "n6_list")

        sign = sb.tile([P, PACK], F32, name="sign")
        twice_nonnegative = sb.tile([P, PACK], F32, name="twice_nonnegative")
        size = sb.tile([P, PACK], F32, name="size")
        nc.gpsimd.tensor_scalar(twice_nonnegative[:], gain[:], 0.0, 2.0, ALU.is_ge, ALU.mult)
        nc.gpsimd.tensor_scalar(sign[:], twice_nonnegative[:], 1.0, -1.0, ALU.mult, ALU.add)
        nc.gpsimd.tensor_tensor(size[:], gain[:], sign[:], ALU.mult)
        quarter = sb.tile([P, 1], F32, name="quarter")
        nc.gpsimd.memset(quarter[:], 0.25)
        warm = sb.tile([P, 1], F32, name="warm")
        nc.scalar.activation(warm[:], quarter[:], ACT.Sqrt)

        y = [sb.tile([P, S if t == LAST else 2 * S], F32, name=f"y{t}") for t in range(PACK)]
        d = [sb.tile([P, S if t == LAST else 2 * S], F32, name=f"d{t}") for t in range(PACK)]

        w12_planes = deal_scales(nc.scalar, w12_rows, 2, "w12_planes")
        w1_plane, w2_plane = w12_planes[:, 0:H], w12_planes[:, H : 2 * H]
        w2_raw = load_words(nc.sync, w2_words, "w2_raw", "raw_a")
        offs_plane = gather_plane(offs_list, "offs")
        hz_plane = gather_plane(hz_list, "hz")
        w1_dealt = deal_words(w1_raw, "w1_dealt")
        offs_codes = sb.tile([P, S], U32, name="offs_codes", align_bytes=64)
        nc.vector.tensor_copy(offs_codes[:], x_table[:].bitcast(U32).indirect(offs_list[:]))
        y_ps = [psum.tile([P, S], F32, name=f"y_ps{t}", tag=f"bank{t}") for t in range(PACK)]
        lead = 2
        for t in range(lead):
            product(y_ps[t][:], w1_dealt, w1_plane, t, offs_codes[:], offs_plane[:])
        w2_dealt = deal_words(w2_raw, "w2_dealt")
        hz_codes = sb.tile([P, S], U32, name="hz_codes", align_bytes=64)
        nc.vector.tensor_copy(hz_codes[:], x_table[:].bitcast(U32).indirect(hz_list[:]))
        d_ps = [psum.tile([P, S], F32, name=f"d_ps{t}", tag=f"bank{PACK + t}") for t in range(PACK)]
        for t in range(PACK):
            product(d_ps[t][:], w2_dealt, w2_plane, t, hz_codes[:], hz_plane[:])
            if t + lead < PACK:
                product(y_ps[t + lead][:], w1_dealt, w1_plane, t + lead, offs_codes[:], offs_plane[:])
        w3_rows = sb.tile([P, H], U8, name="w3_rows", tag="raw_b", align_bytes=64)
        load_scale_rows(nc.sync, w3_scales, w3_rows[:])
        w3_raw = load_words(nc.sync, w3_words, "w3_raw", "raw_a")
        w3_plane = deal_scales(nc.sync, w3_rows, 1, "w3_plane")
        w3_dealt = deal_words(w3_raw, "w3_dealt")

        h = [sb.tile([P, S], F32, name=f"h{t}") for t in range(PACK)]
        h_ps = [
            [psum.tile([P, HALF], F32, name=f"h_ps{half}{t}", tag=f"bank{PACK * half + t}") for t in range(PACK)]
            for half in range(2)
        ]
        larger = sb.tile([P, PACK, S], BF16, name="larger")
        signed = sb.tile([P, PACK, S], BF16, name="signed")
        woven = sb.tile([P, S, PACK], BF16, name="woven", align_bytes=64)
        z_codes = sb.tile([P, S], U32, name="z_codes", align_bytes=64)
        z_plane = sb.tile([P, S], U8, name="z_plane", align_bytes=64)
        sums = {}

        def entries(offsets, lo, hi):
            return offsets[:, lo // 16 : hi // 16]

        def leave_psum(dst, src, t, on_vector):
            if on_vector:
                nc.vector.tensor_scalar(dst[:, 0:S], src[:], size[:, t : t + 1], None, ALU.mult)
            else:
                nc.scalar.activation(dst[:, 0:S], src[:], ACT.Copy, scale=size[:, t : t + 1])

        def fetch(window, offsets, lo, hi, name):
            fetched = sb.tile([P, hi - lo], F32, name=name)
            nc.scalar.activation(fetched[:], window[:].indirect(entries(offsets, lo, hi)), ACT.Copy)
            return fetched

        def add_d(t, lo, hi, which, looked_up, offsets, fetch_on_scalar):
            total = sb.tile([P, hi - lo], F32, name=f"sum{which}{t}_{lo}")
            if fetch_on_scalar:
                fetched = fetch(d[t], offsets, lo, hi, f"d{which}{t}_{lo}")
                nc.vector.tensor_tensor(total[:], fetched[:], looked_up[:], ALU.add)
            else:
                nc.vector.tensor_tensor(total[:], d[t][:].indirect(entries(offsets, lo, hi)), looked_up[:], ALU.add)
            sums[(t, lo, which)] = total

        def take_larger(t, lo, hi):
            nc.vector.tensor_tensor(larger[:, t, lo:hi], sums[(t, lo, "a")][:], sums[(t, lo, "b")][:], ALU.max)

        def apply_sign(t, lo, hi):
            nc.vector.tensor_scalar(signed[:, t, lo:hi], larger[:, t, lo:hi], sign[:, t : t + 1], None, ALU.mult)

        def weave(lo, hi):
            nc.vector.tensor_copy(
                woven[:, lo:hi, :].rearrange("p (c i) t -> p c t i", i=4),
                signed[:, :, lo:hi].rearrange("p t (c i) -> p c t i", i=4),
            )

        def third_product(lo, hi):
            nc.vector.quantize_mx(
                out=z_codes[:, lo:hi].bitcast(FP8X4),
                scales=z_plane[:, lo:hi],
                in_=woven[:, lo:hi, :].rearrange("p c t -> p (c t)"),
            )
            for t in range(PACK):
                out = h_ps[lo // HALF][t][:, lo % HALF : lo % HALF + hi - lo]
                product(out, w3_dealt, w3_plane[:], t, z_codes[:, lo:hi], z_plane[:, lo:hi])

        for t in range(LAST):
            leave_psum(y[t], y_ps[t], t, t == 1)
            ya = fetch(y[t], n1_list, 0, S, f"ya{t}")
            yb = fetch(y[t], n2_list, 0, S, f"yb{t}")
            leave_psum(d[t], d_ps[t], t, t == 0)
            add_d(t, 0, S, "a", ya, n3_list, False)
            if t > 0:
                take_larger(t - 1, 0, S)
            add_d(t, 0, S, "b", yb, n4_list, t == LAST - 1)
            if t > 0:
                apply_sign(t - 1, 0, S)
        leave_psum(y[LAST], y_ps[LAST], LAST, False)
        leave_psum(d[LAST], d_ps[LAST], LAST, False)
        ya = fetch(y[LAST], n1_list, *FIRST, "ya_first")
        add_d(LAST, *FIRST, "a", ya, n3_list, False)
        take_larger(LAST - 1, 0, S)
        yb = fetch(y[LAST], n2_list, *FIRST, "yb_first")
        add_d(LAST, *FIRST, "b", yb, n4_list, True)
        apply_sign(LAST - 1, 0, S)
        take_larger(LAST, *FIRST)
        ya = fetch(y[LAST], n1_list, *SECOND, "ya_second")
        add_d(LAST, *SECOND, "a", ya, n3_list, False)
        apply_sign(LAST, *FIRST)
        yb = fetch(y[LAST], n2_list, *SECOND, "yb_second")
        add_d(LAST, *SECOND, "b", yb, n4_list, True)
        weave(*FIRST)
        take_larger(LAST, *SECOND)
        third_product(*FIRST)
        apply_sign(LAST, *SECOND)
        ya = fetch(y[LAST], n1_list, *THIRD, "ya_third")
        add_d(LAST, *THIRD, "a", ya, n3_list, True)
        weave(*SECOND)
        yb = fetch(y[LAST], n2_list, *THIRD, "yb_third")
        add_d(LAST, *THIRD, "b", yb, n4_list, True)
        third_product(*SECOND)
        take_larger(LAST, *THIRD)
        apply_sign(LAST, *THIRD)
        for t in range(PACK):
            nc.scalar.copy(h[t][:, 0:HALF], h_ps[0][t][:])
        weave(*THIRD)
        third_product(*THIRD)

        out_rows = out_0.rearrange("(p t) c -> p t c", t=PACK)
        rounded = sb.tile([P, S, PACK], BF16, name="rounded", align_bytes=64)
        pair = [sb.tile([P, 2, W], F32, name=f"pair{t}") for t in range(PACK)]
        squares = [sb.tile([P, 2, W], F32, name=f"squares{t}") for t in range(PACK)]
        radicand = [sb.tile([P, W], F32, name=f"radicand{t}") for t in range(PACK)]
        root = [sb.tile([P, W], F32, name=f"root{t}") for t in range(PACK)]
        result = [sb.tile([P, S], F32, name=f"result{t}") for t in range(PACK)]
        staged = sb.tile([P, LAST, S], BF16, name="staged")

        def finish_h(t):
            if t < LAST:
                nc.vector.tensor_copy(h[t][:, HALF:S], h_ps[1][t][:])
            else:
                nc.scalar.copy(h[t][:, HALF:S], h_ps[1][t][:])

        def fetch_pair(t):
            nc.scalar.activation(pair[t][:, 0, :], h[t][:].indirect(n5_list[:]), ACT.Copy, scale=-0.5)
            if t == 0:
                nc.vector.tensor_copy(pair[t][:, 1, :], h[t][:].indirect(n6_list[:]))
            else:
                nc.scalar.activation(pair[t][:, 1, :], h[t][:].indirect(n6_list[:]), ACT.Copy)

        def square(t):
            nc.vector.tensor_tensor(squares[t][:], pair[t][:], pair[t][:], ALU.mult)

        finish_h(0)
        finish_h(1)
        fetch_pair(0)
        fetch_pair(1)
        square(0)
        finish_h(2)
        fetch_pair(2)
        for t in range(PACK):
            nc.vector.scalar_tensor_tensor(
                radicand[t][:], squares[t][:, 0, :], 4.0, squares[t][:, 1, :], ALU.mult, ALU.add
            )
            if t < LAST:
                square(t + 1)
            nc.vector.tensor_tensor(result[t][:].indirect(n6_list[:]), pair[t][:, 1, :], pair[t][:, 0, :], ALU.add)
            nc.scalar.activation(root[t][:], radicand[t][:], ACT.Sqrt, bias=quarter[:])
            nc.scalar.activation(result[t][:].indirect(n5_list[:]), root[t][:], ACT.Copy)
            nc.sync.dma_start(out_rows[:, t, :], result[t][:])
            if t == 0:
                finish_h(LAST)
                fetch_pair(LAST)

        for t in range(LAST):
            nc.vector.tensor_copy(staged[:, t, :], result[t][:])
        nc.vector.tensor_copy(rounded[:, :, 0:LAST], staged[:].rearrange("p t c -> p c t"))
        out_codes = sb.tile([P, S], I32, name="out_codes", align_bytes=64)
        out_plane = sb.tile([P, S], U8, name="out_plane", align_bytes=64)
        out_words = out_1[0].rearrange("p c r -> p (c r)").bitcast(I32)
        halves = [slice(0, HALF), slice(HALF, S)]
        for cols in halves:
            nc.vector.tensor_copy(rounded[:, cols, LAST], result[LAST][:, cols])
        for cols in halves:
            nc.vector.quantize_mx(
                out=out_codes[:, cols].bitcast(FP8X4),
                scales=out_plane[:, cols],
                in_=rounded[:, cols, :].rearrange("p c t -> p (c t)"),
            )
            nc.sync.dma_start(out_words[:, cols], out_codes[:, cols])
        for q in range(4):
            queue = nc.scalar if q % 2 == 0 else nc.sync
            queue.dma_start(
                out_2[0, 4 * q : 4 * q + 4, :].bitcast(I32), out_plane[QUADRANT * q : QUADRANT * q + 4, :].bitcast(I32)
            )
